import numpy as np, ml_dtypes
CORES = [66,74,82,90,194,202,210,218]
N = 8
import mx_ref
NC, G, D = 128, 4, 8
C = np.float32(0.037)
BF = ml_dtypes.bfloat16
def cut(t, i, w=512):
    return t[:, w * i:w * i + w]
def tile(rs):
    return np.stack(rs, axis=2).reshape(128, -1).astype(BF)
def layer(w, X):
    out = []
    for i in range(G):
        for t in range(len(X)):
            p = mx_ref.matmul(mx_ref.quantize(cut(w, len(X) * i + t)), X[t])
            z = p if t == 0 else z + p
        out.append(z)
    return out
def act(Z):
    return [np.maximum(z, 0) * C for z in Z]
def setup_inputs(rng):
    def f(*shape):
        return mx_ref.flush((rng.standard_normal(shape, dtype=np.float32) * np.exp2(rng.integers(-2, 3, shape[:-1] + (1,)))).astype(BF))
    return {"x": f(N, 128, 4 * NC), "w1": f(N, 128, G * 512), "wt": f(N, 128, 3 * 512)}
def setup_inputs_blocks(rng):
    d = setup_inputs(rng)
    for k in ("x", "wt", "w1"): d[k] = mx_ref.spread(d[k], rng, 2)
    return d
def setup_inputs_wide(rng):
    d = setup_inputs(rng)
    for k in ("wt",): d[k] = mx_ref.flush((d[k].astype(np.float32) * np.exp2(rng.integers(-6, 7, (N, 1, 1))).astype(np.float32)).astype(BF))
    return d
def setup_inputs_zeros(rng):
    d = setup_inputs(rng); v = d["x"].reshape(N, 128, -1, 4).copy()
    v[np.broadcast_to((rng.random((N, 1, v.shape[2], 1)) < 0.33), v.shape)] = 0
    d["x"] = v.reshape(d["x"].shape)
    return d
def reference(x, w1, wt):
    h = [tile(act(layer(w1[j], [mx_ref.quantize(x[j])]))) for j in range(N)]
    y = np.zeros((N, 128, NC), np.float32)
    for r in range(N):
        e = np.concatenate([h[(r - 1) % N][:, 4 * (NC - D):], h[r], h[(r + 1) % N][:, :4 * D]], axis=1)
        for t in range(3):
            p = mx_ref.matmul(mx_ref.quantize(cut(wt[r], t)), mx_ref.quantize(e[:, 4 * D * t:4 * D * t + 4 * NC]))
            y[r] = p if t == 0 else y[r] + p
    return {"y": y}

@@ -1,0 +1,108 @@
+from concourse.bass import DstId, RemoteDMATransfer
+from concourse.mybir import dt, AluOpType, ActivationFunctionType
+
+NC, G, D, TAPS = 128, 4, 8, 3
+SD = 4 * D
+OWN = SD
+END = OWN + NC
+WID = END + SD
+FIRST = 3
+CONST = 0.037
+
+SCRATCH = {
+    "xb": ("sbuf", [128, 4 * NC], "bfloat16"),
+    "wb": ("sbuf", [128, G * 512], "bfloat16"),
+    "tb": ("sbuf", [128, TAPS * 512], "bfloat16"),
+    "h": ("sbuf", [128, 4 * NC], "bfloat16"),
+    "xq": ("sbuf", [128, NC], "float8_e4m3fn_x4"),
+    "xs": ("sbuf", [128, NC], "uint8"),
+    "wq": ("sbuf", [128, G * 128], "float8_e4m3fn_x4"),
+    "ws": ("sbuf", [128, G * 128], "uint8"),
+    "tq": ("sbuf", [128, TAPS * 128], "float8_e4m3fn_x4"),
+    "ts": ("sbuf", [128, TAPS * 128], "uint8"),
+    "eq": ("sbuf", [128, WID], "float8_e4m3fn_x4"),
+    "es": ("sbuf", [128, WID], "uint8"),
+    "yb": ("sbuf", [128, NC], "float32"),
+    "z": ("psum", [128, 512 * G], "float32"),
+    "acc": ("psum", [128, 512], "float32"),
+}
+SEMAPHORES = ["ldx", "ldwa", "ldwb", "ldt", "quant", "prod", "half_s", "half_v", "hq", "tapq", "sent",
+              "arr_l", "arr_r", "accd", "copied", "stored"]
+
+
+def rank_program(g, core, T, topo):
+    rank = T.rank_of(core)
+    if rank is None:
+        return
+    n = len(T.cores)
+    s = T.sem
+    left, right = T.cores[(rank - 1) % n], T.cores[(rank + 1) % n]
+
+    cut = FIRST * 512
+    g.sync.dma_start(T.xb[:], T.x[:]).then_inc(s.ldx, 16)
+    g.scalar.dma_start(T.wb[:, 0:cut], T.w1[:, 0:cut]).then_inc(s.ldwa, 16)
+    g.sync.dma_start(T.wb[:, cut:], T.w1[:, cut:]).then_inc(s.ldwb, 16)
+    g.sync.dma_start(T.tb[:], T.wt[:]).then_inc(s.ldt, 16)
+
+    g.vector.wait_ge(s.ldx, 16)
+    g.vector.quantize_mx(T.xq[:], T.xs[:], T.xb[:]).then_inc(s.quant, 1)
+    g.vector.wait_ge(s.ldwa, 16)
+    for i in range(G):
+        if i == FIRST:
+            g.vector.wait_ge(s.ldwb, 16)
+        c = slice(128 * i, 128 * i + 128)
+        g.vector.quantize_mx(T.wq[:, c], T.ws[:, c], T.wb[:, 512 * i:512 * i + 512]).then_inc(s.quant, 1)
+        g.tensor.wait_ge(s.quant, i + 2)
+        z = T.z[:, 512 * i:512 * i + NC]
+        g.tensor.matmul_mx(z, T.wq[:, c], T.ws[:, c], T.xq[:], T.xs[:], True, True).then_inc(s.prod, 1)
+        if i < G - 1:
+            g.scalar.wait_ge(s.prod, i + 1)
+            g.scalar.activation(T.h[:, i:4 * NC:4], z, ActivationFunctionType.Relu, scale=CONST).then_inc(s.half_s, 1)
+        else:
+            g.vector.wait_ge(s.prod, G)
+            g.vector.tensor_scalar(T.h[:, i:4 * NC:4], z, 0.0, CONST, AluOpType.max, AluOpType.mult).then_inc(s.half_v, 1)
+    g.vector.wait_ge(s.half_s, G - 1)
+    g.vector.wait_ge(s.half_v, 1)
+    g.vector.quantize_mx(T.eq[:, OWN:END], T.es[:, OWN:END], T.h[:]).then_inc(s.hq, 1)
+
+    def codes(a):
+        return T.eq[:, a:a + D].bitcast(dt.uint8)
+
+    def scales(a):
+        return T.es[:, a:a + SD]
+
+    moves = []
+    for dst, sem, cs, cd, ss, sd in ((left, s.arr_r, OWN, END, OWN, END),
+                                     (right, s.arr_l, END - D, OWN - D, END - SD, OWN - SD)):
+        moves.append((dst, sem, codes(cs), codes(cd)))
+        moves.append((dst, sem, scales(ss), scales(sd)))
+    allowed = topo.mask(core, left) & topo.mask(core, right)
+    bits = [1 << b for b in range(16) if (allowed >> b) & 1]
+    per = len(bits) // len(moves)
+    transfers = []
+    for k, (dst, sem, src, to) in enumerate(moves):
+        rid, pid = topo.addr(dst, core)
+        transfers.append(RemoteDMATransfer(dst_ids=[DstId(rid=rid, pnc=pid)], dma_engine_mask=sum(bits[per * k:per * k + per]),
+                                           remote_sem=sem, src=src, dst=to))
+    g.wait_ge(s.hq, 1)
+    g.remote_dma_fused(transfers, local_sem=s.sent)
+    g.wait_ge(s.sent, per * len(moves))
+
+    g.vector.wait_ge(s.ldt, 16)
+    g.vector.quantize_mx(T.tq[:], T.ts[:], T.tb[:]).then_inc(s.tapq, 1)
+    order = [1, 2, 0] if topo.mates(core, right) else [1, 0, 2]
+    arrival = {0: s.arr_l, 2: s.arr_r}
+    g.tensor.wait_ge(s.hq, 1)
+    g.tensor.wait_ge(s.tapq, 1)
+    for k, t in enumerate(order):
+        if t in arrival:
+            g.tensor.wait_ge(arrival[t], 2 * per)
+        c, a = slice(128 * t, 128 * t + 128), OWN + D * (t - 1)
+        m = g.tensor.matmul_mx(T.acc[:, 0:NC], T.tq[:, c], T.ts[:, c], T.eq[:, a:a + NC], T.es[:, a:a + NC],
+                               k == 0, k == TAPS - 1)
+    m.then_inc(s.accd, 1)
+    g.vector.wait_ge(s.accd, 1)
+    g.vector.tensor_copy(T.yb[:], T.acc[:, 0:NC]).then_inc(s.copied, 1)
+    g.sync.wait_ge(s.copied, 1)
+    g.sync.dma_start(T.y[:], T.yb[:]).then_inc(s.stored, 16)
+    g.sync.wait_ge(s.stored, 16)

@@ -1,12 +1,12 @@
-from concourse.bass import DstId, RemoteDMATransfer
 from concourse.mybir import dt, AluOpType, ActivationFunctionType
 
 NC, G, D, TAPS = 128, 4, 8, 3
-SD = 4 * D
-OWN = SD
+OWN = 32
 END = OWN + NC
-WID = END + SD
-FIRST = 3
+WID = END + D
+HALF = NC // 2
+PARTS = [(0, 2), (2, 3), (3, 4)]
+EARLY = 2
 CONST = 0.037
 
 SCRATCH = {
@@ -14,20 +14,23 @@ SCRATCH = {
     "wb": ("sbuf", [128, G * 512], "bfloat16"),
     "tb": ("sbuf", [128, TAPS * 512], "bfloat16"),
     "h": ("sbuf", [128, 4 * NC], "bfloat16"),
-    "xq": ("sbuf", [128, NC], "float8_e4m3fn_x4"),
-    "xs": ("sbuf", [128, NC], "uint8"),
+    "he": ("sbuf", [128, 4 * NC], "bfloat16"),
+    "xq": ("sbuf", [128, 2 * NC], "float8_e4m3fn_x4"),
+    "xs": ("sbuf", [128, 2 * NC], "uint8"),
     "wq": ("sbuf", [128, G * 128], "float8_e4m3fn_x4"),
     "ws": ("sbuf", [128, G * 128], "uint8"),
     "tq": ("sbuf", [128, TAPS * 128], "float8_e4m3fn_x4"),
     "ts": ("sbuf", [128, TAPS * 128], "uint8"),
+    "cq": ("sbuf", [128, NC], "float8_e4m3fn_x4"),
+    "cs": ("sbuf", [128, NC], "uint8"),
     "eq": ("sbuf", [128, WID], "float8_e4m3fn_x4"),
     "es": ("sbuf", [128, WID], "uint8"),
     "yb": ("sbuf", [128, NC], "float32"),
     "z": ("psum", [128, 512 * G], "float32"),
     "acc": ("psum", [128, 512], "float32"),
 }
-SEMAPHORES = ["ldx", "ldwa", "ldwb", "ldt", "quant", "prod", "half_s", "half_v", "hq", "tapq", "sent",
-              "arr_l", "arr_r", "accd", "copied", "stored"]
+SEMAPHORES = ["ldx", "ldw0", "ldw1", "ldw2", "ldt", "fill", "quant", "prod", "edge_s", "edge_v", "edgeq", "rest_s",
+              "rest_v", "hq", "tapq", "sent", "arr_l", "arr_r", "accd", "copied", "stored"]
 
 
 def rank_program(g, core, T, topo):
@@ -38,65 +41,88 @@ def rank_program(g, core, T, topo):
     s = T.sem
     left, right = T.cores[(rank - 1) % n], T.cores[(rank + 1) % n]
 
-    cut = FIRST * 512
+    def load_w1(q, k):
+        c = slice(512 * PARTS[k][0], 512 * PARTS[k][1])
+        q.dma_start(T.wb[:, c], T.w1[:, c]).then_inc(s["ldw%d" % k], 16)
+
+    def act_s(out, a, b, i, z, sem):
+        g.scalar.activation(out[:, 4 * a + i:4 * b:4], T.z[:, 512 * i + z:512 * i + z + b - a],
+                            ActivationFunctionType.Relu, scale=CONST).then_inc(sem, 1)
+
+    def act_v(out, a, b, i, z, sem):
+        g.vector.tensor_scalar(out[:, 4 * a + i:4 * b:4], T.z[:, 512 * i + z:512 * i + z + b - a], 0.0, CONST,
+                               AluOpType.max, AluOpType.mult).then_inc(sem, 1)
+
+    lo, hi = HALF - D, HALF + D
+
     g.sync.dma_start(T.xb[:], T.x[:]).then_inc(s.ldx, 16)
-    g.scalar.dma_start(T.wb[:, 0:cut], T.w1[:, 0:cut]).then_inc(s.ldwa, 16)
-    g.sync.dma_start(T.wb[:, cut:], T.w1[:, cut:]).then_inc(s.ldwb, 16)
+    load_w1(g.scalar, 0)
+    load_w1(g.sync, 1)
+    load_w1(g.sync, 2)
     g.sync.dma_start(T.tb[:], T.wt[:]).then_inc(s.ldt, 16)
 
+    g.vector.memset(T.he[:], 0.0).then_inc(s.fill, 1)
     g.vector.wait_ge(s.ldx, 16)
-    g.vector.quantize_mx(T.xq[:], T.xs[:], T.xb[:]).then_inc(s.quant, 1)
-    g.vector.wait_ge(s.ldwa, 16)
-    for i in range(G):
-        if i == FIRST:
-            g.vector.wait_ge(s.ldwb, 16)
-        c = slice(128 * i, 128 * i + 128)
-        g.vector.quantize_mx(T.wq[:, c], T.ws[:, c], T.wb[:, 512 * i:512 * i + 512]).then_inc(s.quant, 1)
-        g.tensor.wait_ge(s.quant, i + 2)
-        z = T.z[:, 512 * i:512 * i + NC]
-        g.tensor.matmul_mx(z, T.wq[:, c], T.ws[:, c], T.xq[:], T.xs[:], True, True).then_inc(s.prod, 1)
-        if i < G - 1:
-            g.scalar.wait_ge(s.prod, i + 1)
-            g.scalar.activation(T.h[:, i:4 * NC:4], z, ActivationFunctionType.Relu, scale=CONST).then_inc(s.half_s, 1)
-        else:
-            g.vector.wait_ge(s.prod, G)
-            g.vector.tensor_scalar(T.h[:, i:4 * NC:4], z, 0.0, CONST, AluOpType.max, AluOpType.mult).then_inc(s.half_v, 1)
-    g.vector.wait_ge(s.half_s, G - 1)
-    g.vector.wait_ge(s.half_v, 1)
-    g.vector.quantize_mx(T.eq[:, OWN:END], T.es[:, OWN:END], T.h[:]).then_inc(s.hq, 1)
+    for k in range(2):
+        c = slice(NC * k, NC * k + NC)
+        g.vector.quantize_mx(T.xq[:, c], T.xs[:, c], T.xb[:]).then_inc(s.quant, 1)
+    turned = slice(HALF, HALF + NC)
+    for k, (first, stop) in enumerate(PARTS):
+        g.vector.wait_ge(s["ldw%d" % k], 16)
+        c = slice(128 * first, 128 * stop)
+        g.vector.quantize_mx(T.wq[:, c], T.ws[:, c], T.wb[:, 512 * first:512 * stop]).then_inc(s.quant, 1)
+        g.tensor.wait_ge(s.quant, k + 3)
+        for i in range(first, stop):
+            c = slice(128 * i, 128 * i + 128)
+            g.tensor.matmul_mx(T.z[:, 512 * i:512 * i + NC], T.wq[:, c], T.ws[:, c], T.xq[:, turned], T.xs[:, turned],
+                               True, True).then_inc(s.prod, 1)
 
-    def codes(a):
-        return T.eq[:, a:a + D].bitcast(dt.uint8)
+    g.scalar.wait_ge(s.fill, 1)
+    g.vector.wait_ge(s.fill, 1)
+    for i in range(EARLY):
+        g.scalar.wait_ge(s.prod, i + 1)
+        act_s(T.he, lo, hi, i, lo, s.edge_s)
+    for i in range(EARLY, G):
+        g.vector.wait_ge(s.prod, i + 1)
+        act_v(T.he, lo, hi, i, lo, s.edge_v)
+    g.vector.wait_ge(s.edge_s, EARLY)
+    g.vector.wait_ge(s.edge_v, G - EARLY)
+    g.vector.quantize_mx(T.cq[:], T.cs[:], T.he[:]).then_inc(s.edgeq, 1)
 
-    def scales(a):
-        return T.es[:, a:a + SD]
-
-    moves = []
-    for dst, sem, cs, cd, ss, sd in ((left, s.arr_r, OWN, END, OWN, END),
-                                     (right, s.arr_l, END - D, OWN - D, END - SD, OWN - SD)):
-        moves.append((dst, sem, codes(cs), codes(cd)))
-        moves.append((dst, sem, scales(ss), scales(sd)))
-    allowed = topo.mask(core, left) & topo.mask(core, right)
-    bits = [1 << b for b in range(16) if (allowed >> b) & 1]
-    per = len(bits) // len(moves)
-    transfers = []
-    for k, (dst, sem, src, to) in enumerate(moves):
+    sides = [(left, s.arr_r, HALF, END), (right, s.arr_l, HALF - D, OWN - D)]
+    if topo.mates(core, left):
+        sides.reverse()
+    g.wait_ge(s.edgeq, 1)
+    total = 0
+    for dst, sem, a, b in sides:
+        mask = topo.mask(core, dst)
+        count = bin(mask).count("1")
         rid, pid = topo.addr(dst, core)
-        transfers.append(RemoteDMATransfer(dst_ids=[DstId(rid=rid, pnc=pid)], dma_engine_mask=sum(bits[per * k:per * k + per]),
-                                           remote_sem=sem, src=src, dst=to))
-    g.wait_ge(s.hq, 1)
-    g.remote_dma_fused(transfers, local_sem=s.sent)
-    g.wait_ge(s.sent, per * len(moves))
+        for to, src in ((T.eq[:, b:b + D].bitcast(dt.uint8), T.cq[:, a:a + D].bitcast(dt.uint8)),
+                        (T.es[:, b:b + D], T.cs[:, a:a + D])):
+            g.remote_dma(to, src, remote_sem=sem, local_sem=s.sent, pid=pid, routing_id=rid, dma_engine_mask=mask)
+            total += count
+    g.wait_ge(s.sent, total)
 
+    for i in range(EARLY):
+        act_s(T.h, HALF, NC, i, 0, s.rest_s)
+        act_s(T.h, 0, HALF, i, HALF, s.rest_s)
+    for i in range(EARLY, G):
+        act_v(T.h, HALF, NC, i, 0, s.rest_v)
+        act_v(T.h, 0, HALF, i, HALF, s.rest_v)
     g.vector.wait_ge(s.ldt, 16)
     g.vector.quantize_mx(T.tq[:], T.ts[:], T.tb[:]).then_inc(s.tapq, 1)
+    g.vector.wait_ge(s.rest_s, 2 * EARLY)
+    g.vector.wait_ge(s.rest_v, 2 * (G - EARLY))
+    g.vector.quantize_mx(T.eq[:, OWN:END], T.es[:, OWN:END], T.h[:]).then_inc(s.hq, 1)
+
     order = [1, 2, 0] if topo.mates(core, right) else [1, 0, 2]
     arrival = {0: s.arr_l, 2: s.arr_r}
-    g.tensor.wait_ge(s.hq, 1)
     g.tensor.wait_ge(s.tapq, 1)
+    g.tensor.wait_ge(s.hq, 1)
     for k, t in enumerate(order):
         if t in arrival:
-            g.tensor.wait_ge(arrival[t], 2 * per)
+            g.tensor.wait_ge(arrival[t], 2 * count)
         c, a = slice(128 * t, 128 * t + 128), OWN + D * (t - 1)
         m = g.tensor.matmul_mx(T.acc[:, 0:NC], T.tq[:, c], T.ts[:, c], T.eq[:, a:a + NC], T.es[:, a:a + NC],
                                k == 0, k == TAPS - 1)

from concourse.mybir import dt, AluOpType, ActivationFunctionType

NC, G, D, TAPS = 128, 4, 8, 3
OWN = 32
END = OWN + NC
WID = END + D
HALF = NC // 2
PARTS = [(0, 2), (2, 3), (3, 4)]
EARLY = 2
CONST = 0.037

SCRATCH = {
    "xb": ("sbuf", [128, 4 * NC], "bfloat16"),
    "wb": ("sbuf", [128, G * 512], "bfloat16"),
    "tb": ("sbuf", [128, TAPS * 512], "bfloat16"),
    "h": ("sbuf", [128, 4 * NC], "bfloat16"),
    "he": ("sbuf", [128, 4 * NC], "bfloat16"),
    "xq": ("sbuf", [128, 2 * NC], "float8_e4m3fn_x4"),
    "xs": ("sbuf", [128, 2 * NC], "uint8"),
    "wq": ("sbuf", [128, G * 128], "float8_e4m3fn_x4"),
    "ws": ("sbuf", [128, G * 128], "uint8"),
    "tq": ("sbuf", [128, TAPS * 128], "float8_e4m3fn_x4"),
    "ts": ("sbuf", [128, TAPS * 128], "uint8"),
    "cq": ("sbuf", [128, NC], "float8_e4m3fn_x4"),
    "cs": ("sbuf", [128, NC], "uint8"),
    "eq": ("sbuf", [128, WID], "float8_e4m3fn_x4"),
    "es": ("sbuf", [128, WID], "uint8"),
    "yb": ("sbuf", [128, NC], "float32"),
    "z": ("psum", [128, 512 * G], "float32"),
    "acc": ("psum", [128, 512], "float32"),
}
SEMAPHORES = ["ldx", "ldw0", "ldw1", "ldw2", "ldt", "fill", "quant", "prod", "edge_s", "edge_v", "edgeq", "rest_s",
              "rest_v", "hq", "tapq", "sent", "arr_l", "arr_r", "accd", "copied", "stored"]


def rank_program(g, core, T, topo):
    rank = T.rank_of(core)
    if rank is None:
        return
    n = len(T.cores)
    s = T.sem
    left, right = T.cores[(rank - 1) % n], T.cores[(rank + 1) % n]

    def load_w1(q, k):
        c = slice(512 * PARTS[k][0], 512 * PARTS[k][1])
        q.dma_start(T.wb[:, c], T.w1[:, c]).then_inc(s["ldw%d" % k], 16)

    def act_s(out, a, b, i, z, sem):
        g.scalar.activation(out[:, 4 * a + i:4 * b:4], T.z[:, 512 * i + z:512 * i + z + b - a],
                            ActivationFunctionType.Relu, scale=CONST).then_inc(sem, 1)

    def act_v(out, a, b, i, z, sem):
        g.vector.tensor_scalar(out[:, 4 * a + i:4 * b:4], T.z[:, 512 * i + z:512 * i + z + b - a], 0.0, CONST,
                               AluOpType.max, AluOpType.mult).then_inc(sem, 1)

    lo, hi = HALF - D, HALF + D

    g.sync.dma_start(T.xb[:], T.x[:]).then_inc(s.ldx, 16)
    load_w1(g.scalar, 0)
    load_w1(g.sync, 1)
    load_w1(g.sync, 2)
    g.sync.dma_start(T.tb[:], T.wt[:]).then_inc(s.ldt, 16)

    g.vector.memset(T.he[:], 0.0).then_inc(s.fill, 1)
    g.vector.wait_ge(s.ldx, 16)
    for k in range(2):
        c = slice(NC * k, NC * k + NC)
        g.vector.quantize_mx(T.xq[:, c], T.xs[:, c], T.xb[:]).then_inc(s.quant, 1)
    turned = slice(HALF, HALF + NC)
    for k, (first, stop) in enumerate(PARTS):
        g.vector.wait_ge(s["ldw%d" % k], 16)
        c = slice(128 * first, 128 * stop)
        g.vector.quantize_mx(T.wq[:, c], T.ws[:, c], T.wb[:, 512 * first:512 * stop]).then_inc(s.quant, 1)
        g.tensor.wait_ge(s.quant, k + 3)
        for i in range(first, stop):
            c = slice(128 * i, 128 * i + 128)
            g.tensor.matmul_mx(T.z[:, 512 * i:512 * i + NC], T.wq[:, c], T.ws[:, c], T.xq[:, turned], T.xs[:, turned],
                               True, True).then_inc(s.prod, 1)

    g.scalar.wait_ge(s.fill, 1)
    g.vector.wait_ge(s.fill, 1)
    for i in range(EARLY):
        g.scalar.wait_ge(s.prod, i + 1)
        act_s(T.he, lo, hi, i, lo, s.edge_s)
    for i in range(EARLY, G):
        g.vector.wait_ge(s.prod, i + 1)
        act_v(T.he, lo, hi, i, lo, s.edge_v)
    g.vector.wait_ge(s.edge_s, EARLY)
    g.vector.wait_ge(s.edge_v, G - EARLY)
    g.vector.quantize_mx(T.cq[:], T.cs[:], T.he[:]).then_inc(s.edgeq, 1)

    sides = [(left, s.arr_r, HALF, END), (right, s.arr_l, HALF - D, OWN - D)]
    if topo.mates(core, left):
        sides.reverse()
    g.wait_ge(s.edgeq, 1)
    total = 0
    for dst, sem, a, b in sides:
        mask = topo.mask(core, dst)
        count = bin(mask).count("1")
        rid, pid = topo.addr(dst, core)
        for to, src in ((T.eq[:, b:b + D].bitcast(dt.uint8), T.cq[:, a:a + D].bitcast(dt.uint8)),
                        (T.es[:, b:b + D], T.cs[:, a:a + D])):
            g.remote_dma(to, src, remote_sem=sem, local_sem=s.sent, pid=pid, routing_id=rid, dma_engine_mask=mask)
            total += count
    g.wait_ge(s.sent, total)

    for i in range(EARLY):
        act_s(T.h, HALF, NC, i, 0, s.rest_s)
        act_s(T.h, 0, HALF, i, HALF, s.rest_s)
    for i in range(EARLY, G):
        act_v(T.h, HALF, NC, i, 0, s.rest_v)
        act_v(T.h, 0, HALF, i, HALF, s.rest_v)
    g.vector.wait_ge(s.ldt, 16)
    g.vector.quantize_mx(T.tq[:], T.ts[:], T.tb[:]).then_inc(s.tapq, 1)
    g.vector.wait_ge(s.rest_s, 2 * EARLY)
    g.vector.wait_ge(s.rest_v, 2 * (G - EARLY))
    g.vector.quantize_mx(T.eq[:, OWN:END], T.es[:, OWN:END], T.h[:]).then_inc(s.hq, 1)

    order = [1, 2, 0] if topo.mates(core, right) else [1, 0, 2]
    arrival = {0: s.arr_l, 2: s.arr_r}
    g.tensor.wait_ge(s.tapq, 1)
    g.tensor.wait_ge(s.hq, 1)
    for k, t in enumerate(order):
        if t in arrival:
            g.tensor.wait_ge(arrival[t], 2 * count)
        c, a = slice(128 * t, 128 * t + 128), OWN + D * (t - 1)
        m = g.tensor.matmul_mx(T.acc[:, 0:NC], T.tq[:, c], T.ts[:, c], T.eq[:, a:a + NC], T.es[:, a:a + NC],
                               k == 0, k == TAPS - 1)
    m.then_inc(s.accd, 1)
    g.vector.wait_ge(s.accd, 1)
    g.vector.tensor_copy(T.yb[:], T.acc[:, 0:NC]).then_inc(s.copied, 1)
    g.sync.wait_ge(s.copied, 1)
    g.sync.dma_start(T.y[:], T.yb[:]).then_inc(s.stored, 16)
    g.sync.wait_ge(s.stored, 16)
